import numpy as np, ml_dtypes
CORES = [35,38,43,46]
N = 4
import mx_ref
NC = 384
BF = ml_dtypes.bfloat16
def setup_inputs(rng):
    def f(*shape):
        return mx_ref.flush((rng.standard_normal(shape, dtype=np.float32) * np.exp2(rng.integers(-2, 3, shape[:-1] + (1,)))).astype(BF))
    return {"x": f(N, 128, 512), "w": f(N, 128, 4 * NC)}
def setup_inputs_blocks(rng):
    d = setup_inputs(rng)
    for k in ("x", "w"): d[k] = mx_ref.spread(d[k], rng, 4)
    return d
def setup_inputs_wide(rng):
    d = setup_inputs(rng)
    for k in ("x", "w"): d[k] = mx_ref.flush((d[k].astype(np.float32) * np.exp2(rng.integers(-6, 7, (N, 1, 1))).astype(np.float32)).astype(BF))
    return d
def setup_inputs_near(rng):
    d = setup_inputs(rng); v = d["w"].astype(np.float32).reshape(N, 128, -1, 4)
    d["w"] = mx_ref.flush((v[:1, :, :1] + v / 64).reshape(d["w"].shape).astype(BF))
    return d
def setup_inputs_twins(rng):
    d = setup_inputs(rng); v = d["w"].reshape(N, 128, -1, 4).copy(); a, b = rng.permutation(N)[:2]; i, j, k = rng.integers(0, v.shape[2], 3)
    v[a, :, i] = (v[a, :, i].astype(np.float32) * 8).astype(BF); v[a, :, j] = v[a, :, i]; v[b, :, k] = v[a, :, i]
    d["w"] = v.reshape(d["w"].shape)
    return d
def reference(x, w):
    W = [mx_ref.quantize(w[r]) for r in range(N)]
    y = np.zeros((N, 128, 2), np.float32)
    for j in range(N):
        X = mx_ref.quantize(x[j])
        L = np.concatenate([mx_ref.matmul(X, W[r]) for r in range(N)], axis=1)
        y[j][:, 0] = L.max(axis=1); y[j][:, 1] = L.argmax(axis=1)
    return {"y": y}

@@ -1,0 +1,135 @@
+from concourse.bass import DstId, RemoteDMATransfer
+from concourse.mybir import dt, AluOpType, AxisListType, ActivationFunctionType
+
+NT = 128
+NC = 384
+SLOT = 400
+BIG = 8192.0
+LOW = -1.0e29
+
+SCRATCH = {
+    "xt": ("sbuf", [128, 4 * NT], "bfloat16"),
+    "wt": ("sbuf", [128, 4 * NC], "bfloat16"),
+    "xc": ("sbuf", [128, 4 * NT], "float8_e4m3fn_x4"),
+    "xs": ("sbuf", [128, 4 * NT], "uint8"),
+    "wc": ("sbuf", [128, NC], "float8_e4m3fn_x4"),
+    "ws": ("sbuf", [128, NC], "uint8"),
+    "ps": ("psum", [128, 4 * 512], "float32"),
+    "low": ("sbuf", [128, NC], "bfloat16"),
+    "run": ("sbuf", [128, 4 * SLOT], "float32"),
+    "land": ("sbuf", [128, 4 * SLOT], "float32"),
+    "junk": ("sbuf", [128, 4 * NC], "bfloat16"),
+    "off": ("sbuf", [128, 4], "float32"),
+    "idx": ("sbuf", [128, 4], "float32"),
+    "pen": ("sbuf", [128, 4], "float32"),
+    "best": ("sbuf", [128, 8], "float32"),
+}
+SEMAPHORES = (["ldx", "ldw", "qx", "qw", "low", "off", "sent", "res", "gmax", "idx", "pen", "fin", "st"]
+              + ["arr%d" % k for k in range(4)] + ["mm%d" % k for k in range(4)]
+              + ["sc%d" % k for k in range(4)] + ["ac%d" % k for k in range(4)])
+
+
+def rank_program(g, core, T, topo):
+    me = T.rank_of(core)
+    if me is None:
+        return
+    cores = T.cores
+    n = len(cores)
+
+    def dst(c):
+        rid, pid, _ = topo.addr(c)
+        return DstId(rid=rid, pnc=pid)
+
+    def engines(m):
+        return [e for e in range(m.bit_length()) if (m >> e) & 1]
+
+    def mask(es):
+        return sum(1 << e for e in es)
+
+    others = [r for r in range(n) if r != me]
+    near = [r for r in others if topo.chip(cores[r]) == topo.chip(core)]
+    far = [r for r in others if r not in near]
+    far.sort(key=lambda r: topo.die(cores[r]) != topo.die(core))
+    far_es = engines(topo.mask(core, cores[far[0]]))
+    near_es = [e for e in engines(topo.mask(core, cores[near[0]])) if e not in far_es]
+    half = len(far_es) // len(far)
+    order = [me] + near + far
+
+    g.sync.dma_start(T.xt[:], T.x[:]).then_inc(T.sem.ldx, 16)
+    g.sync.dma_start(T.wt[:], T.w[:]).then_inc(T.sem.ldw, 16)
+
+    def codes(r):
+        return T.xc[:, NT * r:NT * (r + 1)]
+
+    def plane(r):
+        return T.xs[:, NT * r:NT * (r + 1)]
+
+    g.iota(T.off[:], [[-NC, n]], NC * (n - 1), 0, allow_small_or_imprecise_dtypes=True).then_inc(T.sem.off, 1)
+    g.wait_ge(T.sem.qx, 1)
+    arr = T.sem["arr%d" % me]
+    for piece in (codes(me).bitcast(dt.uint8), plane(me)):
+        g.remote_dma_fused([
+            RemoteDMATransfer(dst_ids=[dst(cores[r]) for r in far], dma_engine_mask=mask(far_es), remote_sem=arr,
+                              srcs=[piece], dsts=[piece for r in far]),
+            RemoteDMATransfer(dst_ids=[dst(cores[r]) for r in near], dma_engine_mask=mask(near_es), remote_sem=arr,
+                              srcs=[piece], dsts=[piece for r in near]),
+        ], local_sem=T.sem.sent)
+
+    def record(r, a, b):
+        if r == me:
+            q = SLOT * (n - 1 - me)
+            return T.land[:, q + a:q + b]
+        return T.run[:, SLOT * r + a:SLOT * r + b]
+
+    g.vector.memset(T.low[:], LOW).then_inc(T.sem.low, 1)
+    g.vector.wait_ge(T.sem.ldx, 16)
+    g.vector.quantize_mx(codes(me), plane(me), T.xt[:]).then_inc(T.sem.qx, 1)
+    g.vector.wait_ge(T.sem.ldw, 16)
+    g.vector.quantize_mx(T.wc[:], T.ws[:], T.wt[:]).then_inc(T.sem.qw, 1)
+    g.vector.wait_ge(T.sem.low, 1)
+
+    g.tensor.wait_ge(T.sem.qx, 1)
+    g.tensor.wait_ge(T.sem.qw, 1)
+    for k, r in enumerate(order):
+        if r in near:
+            g.tensor.wait_ge(T.sem["arr%d" % r], 2 * len(near_es))
+        elif r in far:
+            g.tensor.wait_ge(T.sem["arr%d" % r], 2 * len(far_es))
+        bank = T.ps[:, 512 * k:512 * k + NC]
+        g.tensor.matmul_mx(bank, codes(r), plane(r), T.wc[:], T.ws[:], True, True).then_inc(T.sem["mm%d" % k], 1)
+        g.vector.wait_ge(T.sem["mm%d" % k], 1)
+        g.vector.tensor_tensor_scan(record(r, 0, NC), bank, T.low[:], LOW, AluOpType.max,
+                                    AluOpType.max).then_inc(T.sem["sc%d" % k], 1)
+        g.scalar.wait_ge(T.sem["sc%d" % k], 1)
+        g.scalar.activation(T.junk[:, NC * k:NC * (k + 1)], record(r, 0, NC), ActivationFunctionType.Sign,
+                            bias=record(r, NC - 1, NC), scale=-1.0,
+                            accum_out=record(r, NC, NC + 1)).then_inc(T.sem["ac%d" % k], 1)
+
+    q = SLOT * (n - 1 - me)
+    home = T.land[:, q + NC - 1:q + NC + 1]
+    for k in range(1, n):
+        g.wait_ge(T.sem["ac%d" % k], 1)
+    moves = [(r, far_es[half * i:half * (i + 1)]) for i, r in enumerate(far)] + [(r, near_es) for r in near]
+    g.remote_dma_fused([
+        RemoteDMATransfer(dst_ids=[dst(cores[r])], dma_engine_mask=mask(es), remote_sem=T.sem.res,
+                          srcs=[record(r, NC - 1, NC + 1)], dsts=[home]) for r, es in moves
+    ], local_sem=T.sem.sent)
+    g.wait_ge(T.sem.sent, 3 * (len(far_es) + len(near_es)))
+
+    top = T.land[:, NC - 1:n * SLOT:SLOT]
+    pos = T.land[:, NC:n * SLOT:SLOT]
+    g.vector.wait_ge(T.sem.off, 1)
+    g.vector.wait_ge(T.sem.sc0, 1)
+    g.vector.wait_ge(T.sem.ac0, 1)
+    g.vector.wait_ge(T.sem.res, half * len(far) + len(near_es))
+    g.vector.tensor_reduce(T.best[:, 6:7], top, AxisListType.X, AluOpType.max).then_inc(T.sem.gmax, 1)
+    g.vector.tensor_tensor(T.idx[:], pos, T.off[:], AluOpType.add).then_inc(T.sem.idx, 1)
+    g.vector.wait_ge(T.sem.gmax, 1)
+    g.vector.tensor_scalar(T.pen[:], top, T.best[:, 6:7], BIG, AluOpType.is_lt, AluOpType.mult).then_inc(T.sem.pen, 1)
+    g.vector.wait_ge(T.sem.idx, 1)
+    g.vector.wait_ge(T.sem.pen, 1)
+    g.vector.tensor_tensor_scan(T.best[:, 1:8:2], T.pen[:], T.idx[:], BIG, AluOpType.min,
+                                AluOpType.max).then_inc(T.sem.fin, 1)
+    g.sync.wait_ge(T.sem.fin, 1)
+    g.sync.dma_start(T.y[:], T.best[:, 6:8]).then_inc(T.sem.st, 16)
+    g.sync.wait_ge(T.sem.st, 16)

@@ -3,8 +3,11 @@ from concourse.mybir import dt, AluOpType, AxisListType, ActivationFunctionType
 
 NT = 128
 NC = 384
+HALF = 192
 SLOT = 400
+PAIR = 12
 BIG = 8192.0
+NONE = 4 * BIG
 LOW = -1.0e29
 
 SCRATCH = {
@@ -14,17 +17,16 @@ SCRATCH = {
     "xs": ("sbuf", [128, 4 * NT], "uint8"),
     "wc": ("sbuf", [128, NC], "float8_e4m3fn_x4"),
     "ws": ("sbuf", [128, NC], "uint8"),
-    "ps": ("psum", [128, 4 * 512], "float32"),
+    "ps": ("psum", [128, 5 * 512], "float32"),
     "low": ("sbuf", [128, NC], "bfloat16"),
     "run": ("sbuf", [128, 4 * SLOT], "float32"),
-    "land": ("sbuf", [128, 4 * SLOT], "float32"),
     "junk": ("sbuf", [128, 4 * NC], "bfloat16"),
-    "off": ("sbuf", [128, 4], "float32"),
-    "idx": ("sbuf", [128, 4], "float32"),
-    "pen": ("sbuf", [128, 4], "float32"),
-    "best": ("sbuf", [128, 8], "float32"),
+    "land": ("sbuf", [128, 4 * PAIR], "float32"),
+    "step": ("sbuf", [128, 12], "float32"),
+    "best": ("sbuf", [128, 24], "float32"),
 }
-SEMAPHORES = (["ldx", "ldw", "qx", "qw", "low", "off", "sent", "res", "gmax", "idx", "pen", "fin", "st"]
+SEMAPHORES = (["ldx", "ldw", "qx", "qw", "low", "const", "sent", "own", "pair", "top", "res", "gmax", "step", "fin",
+               "st", "mmh", "sch"]
               + ["arr%d" % k for k in range(4)] + ["mm%d" % k for k in range(4)]
               + ["sc%d" % k for k in range(4)] + ["ac%d" % k for k in range(4)])
 
@@ -35,6 +37,7 @@ def rank_program(g, core, T, topo):
         return
     cores = T.cores
     n = len(cores)
+    sem = T.sem
 
     def dst(c):
         rid, pid, _ = topo.addr(c)
@@ -50,13 +53,11 @@ def rank_program(g, core, T, topo):
     near = [r for r in others if topo.chip(cores[r]) == topo.chip(core)]
     far = [r for r in others if r not in near]
     far.sort(key=lambda r: topo.die(cores[r]) != topo.die(core))
-    far_es = engines(topo.mask(core, cores[far[0]]))
-    near_es = [e for e in engines(topo.mask(core, cores[near[0]])) if e not in far_es]
-    half = len(far_es) // len(far)
-    order = [me] + near + far
-
-    g.sync.dma_start(T.xt[:], T.x[:]).then_inc(T.sem.ldx, 16)
-    g.sync.dma_start(T.wt[:], T.w[:]).then_inc(T.sem.ldw, 16)
+    near, (far1, far2) = near[0], far
+    far_es = engines(topo.mask(core, cores[far1]))
+    near_es = [e for e in engines(topo.mask(core, cores[near])) if e not in far_es]
+    es = {far1: far_es, far2: far_es, near: near_es}
+    order = [me, far1, near, far2]
 
     def codes(r):
         return T.xc[:, NT * r:NT * (r + 1)]
@@ -64,72 +65,97 @@ def rank_program(g, core, T, topo):
     def plane(r):
         return T.xs[:, NT * r:NT * (r + 1)]
 
-    g.iota(T.off[:], [[-NC, n]], NC * (n - 1), 0, allow_small_or_imprecise_dtypes=True).then_inc(T.sem.off, 1)
-    g.wait_ge(T.sem.qx, 1)
-    arr = T.sem["arr%d" % me]
-    for piece in (codes(me).bitcast(dt.uint8), plane(me)):
-        g.remote_dma_fused([
-            RemoteDMATransfer(dst_ids=[dst(cores[r]) for r in far], dma_engine_mask=mask(far_es), remote_sem=arr,
-                              srcs=[piece], dsts=[piece for r in far]),
-            RemoteDMATransfer(dst_ids=[dst(cores[r]) for r in near], dma_engine_mask=mask(near_es), remote_sem=arr,
-                              srcs=[piece], dsts=[piece for r in near]),
-        ], local_sem=T.sem.sent)
-
     def record(r, a, b):
-        if r == me:
-            q = SLOT * (n - 1 - me)
-            return T.land[:, q + a:q + b]
         return T.run[:, SLOT * r + a:SLOT * r + b]
 
-    g.vector.memset(T.low[:], LOW).then_inc(T.sem.low, 1)
-    g.vector.wait_ge(T.sem.ldx, 16)
-    g.vector.quantize_mx(codes(me), plane(me), T.xt[:]).then_inc(T.sem.qx, 1)
-    g.vector.wait_ge(T.sem.ldw, 16)
-    g.vector.quantize_mx(T.wc[:], T.ws[:], T.wt[:]).then_inc(T.sem.qw, 1)
-    g.vector.wait_ge(T.sem.low, 1)
+    def send(r, src, out, to):
+        return RemoteDMATransfer(dst_ids=[dst(cores[r])], dma_engine_mask=mask(es[r]), remote_sem=to,
+                                 srcs=[src], dsts=[out])
 
-    g.tensor.wait_ge(T.sem.qx, 1)
-    g.tensor.wait_ge(T.sem.qw, 1)
+    g.sync.dma_start(T.xt[:], T.x[:]).then_inc(sem.ldx, 16)
+    g.sync.dma_start(T.wt[:], T.w[:]).then_inc(sem.ldw, 16)
+
+    g.wait_ge(sem.qx, 1)
+    sent = 0
+    for group in ((far1,), (far2, near)):
+        for piece in (codes(me).bitcast(dt.uint8), plane(me)):
+            g.remote_dma_fused([send(r, piece, piece, sem["arr%d" % me]) for r in group], local_sem=sem.sent)
+            sent += sum(len(es[r]) for r in group)
+
+    g.vector.memset(T.low[:], LOW).then_inc(sem.low, 1)
+    g.vector.wait_ge(sem.ldx, 16)
+    g.vector.quantize_mx(codes(me), plane(me), T.xt[:]).then_inc(sem.qx, 1)
+    for k in range(n):
+        g.vector.memset(T.land[:, PAIR * k + 4:PAIR * (k + 1)], NONE).then_inc(sem.const, 1)
+    g.vector.memset(T.step[:, 2:11:3], float(-NC)).then_inc(sem.const, 1)
+    g.vector.memset(T.step[:, 11:12], float(NC * (n - 1))).then_inc(sem.const, 1)
+    g.vector.wait_ge(sem.ldw, 16)
+    g.vector.quantize_mx(T.wc[:], T.ws[:], T.wt[:]).then_inc(sem.qw, 1)
+    g.vector.wait_ge(sem.low, 1)
+
+    def scan(r, bank, a, b, first, done):
+        g.vector.tensor_tensor_scan(record(r, a, b), bank, T.low[:, a:b], first, AluOpType.max,
+                                    AluOpType.max).then_inc(done, 1)
+
+    g.tensor.wait_ge(sem.qx, 1)
+    g.tensor.wait_ge(sem.qw, 1)
     for k, r in enumerate(order):
-        if r in near:
-            g.tensor.wait_ge(T.sem["arr%d" % r], 2 * len(near_es))
-        elif r in far:
-            g.tensor.wait_ge(T.sem["arr%d" % r], 2 * len(far_es))
-        bank = T.ps[:, 512 * k:512 * k + NC]
-        g.tensor.matmul_mx(bank, codes(r), plane(r), T.wc[:], T.ws[:], True, True).then_inc(T.sem["mm%d" % k], 1)
-        g.vector.wait_ge(T.sem["mm%d" % k], 1)
-        g.vector.tensor_tensor_scan(record(r, 0, NC), bank, T.low[:], LOW, AluOpType.max,
-                                    AluOpType.max).then_inc(T.sem["sc%d" % k], 1)
-        g.scalar.wait_ge(T.sem["sc%d" % k], 1)
+        if r != me:
+            g.tensor.wait_ge(sem["arr%d" % r], 2 * len(es[r]))
+        if r != far2:
+            bank = T.ps[:, 512 * k:512 * k + NC]
+            g.tensor.matmul_mx(bank, codes(r), plane(r), T.wc[:], T.ws[:], True, True).then_inc(sem["mm%d" % k], 1)
+            g.vector.wait_ge(sem["mm%d" % k], 1)
+            scan(r, bank, 0, NC, LOW, sem["sc%d" % k])
+        else:
+            b0, b1 = T.ps[:, 512 * k:512 * k + HALF], T.ps[:, 512 * (k + 1):512 * (k + 1) + NC - HALF]
+            g.tensor.matmul_mx(b0, codes(r), plane(r), T.wc[:, 0:HALF], T.ws[:, 0:HALF], True,
+                               True).then_inc(sem.mmh, 1)
+            g.tensor.matmul_mx(b1, codes(r), plane(r), T.wc[:, HALF:NC], T.ws[:, HALF:NC], True,
+                               True).then_inc(sem["mm%d" % k], 1)
+            g.vector.wait_ge(sem.mmh, 1)
+            scan(r, b0, 0, HALF, LOW, sem.sch)
+            g.vector.wait_ge(sem["mm%d" % k], 1)
+            g.vector.wait_ge(sem.sch, 1)
+            scan(r, b1, HALF, NC, record(r, HALF - 1, HALF), sem["sc%d" % k])
+        g.scalar.wait_ge(sem["sc%d" % k], 1)
         g.scalar.activation(T.junk[:, NC * k:NC * (k + 1)], record(r, 0, NC), ActivationFunctionType.Sign,
                             bias=record(r, NC - 1, NC), scale=-1.0,
-                            accum_out=record(r, NC, NC + 1)).then_inc(T.sem["ac%d" % k], 1)
+                            accum_out=record(r, NC, NC + 1)).then_inc(sem["ac%d" % k], 1)
+        if r == me:
+            g.scalar.wait_ge(sem["ac%d" % k], 1)
+            g.scalar.activation(T.land[:, PAIR * me:PAIR * me + 2], record(r, NC - 1, NC + 1),
+                                ActivationFunctionType.Copy).then_inc(sem.own, 1)
 
-    q = SLOT * (n - 1 - me)
-    home = T.land[:, q + NC - 1:q + NC + 1]
-    for k in range(1, n):
-        g.wait_ge(T.sem["ac%d" % k], 1)
-    moves = [(r, far_es[half * i:half * (i + 1)]) for i, r in enumerate(far)] + [(r, near_es) for r in near]
-    g.remote_dma_fused([
-        RemoteDMATransfer(dst_ids=[dst(cores[r])], dma_engine_mask=mask(es), remote_sem=T.sem.res,
-                          srcs=[record(r, NC - 1, NC + 1)], dsts=[home]) for r, es in moves
-    ], local_sem=T.sem.sent)
-    g.wait_ge(T.sem.sent, 3 * (len(far_es) + len(near_es)))
+    at = PAIR * me
+    g.wait_ge(sem.ac1, 1)
+    g.remote_dma_fused([send(far1, record(far1, NC - 1, NC + 1), T.land[:, at:at + 2], sem.pair)],
+                       local_sem=sem.sent)
+    g.wait_ge(sem.sc2, 1)
+    g.wait_ge(sem.sc3, 1)
+    g.remote_dma_fused([send(r, record(r, NC - 1, NC), T.land[:, at:at + 1], sem.top) for r in (far2, near)],
+                       local_sem=sem.sent)
+    g.wait_ge(sem.ac2, 1)
+    g.wait_ge(sem.ac3, 1)
+    g.remote_dma_fused([send(r, record(r, NC, NC + 1), T.land[:, at + 1:at + 2], sem.res) for r in (far2, near)],
+                       local_sem=sem.sent)
+    late = len(far_es) + len(near_es)
+    g.wait_ge(sem.sent, sent + len(far_es) + 2 * late)
 
-    top = T.land[:, NC - 1:n * SLOT:SLOT]
-    pos = T.land[:, NC:n * SLOT:SLOT]
-    g.vector.wait_ge(T.sem.off, 1)
-    g.vector.wait_ge(T.sem.sc0, 1)
-    g.vector.wait_ge(T.sem.ac0, 1)
-    g.vector.wait_ge(T.sem.res, half * len(far) + len(near_es))
-    g.vector.tensor_reduce(T.best[:, 6:7], top, AxisListType.X, AluOpType.max).then_inc(T.sem.gmax, 1)
-    g.vector.tensor_tensor(T.idx[:], pos, T.off[:], AluOpType.add).then_inc(T.sem.idx, 1)
-    g.vector.wait_ge(T.sem.gmax, 1)
-    g.vector.tensor_scalar(T.pen[:], top, T.best[:, 6:7], BIG, AluOpType.is_lt, AluOpType.mult).then_inc(T.sem.pen, 1)
-    g.vector.wait_ge(T.sem.idx, 1)
-    g.vector.wait_ge(T.sem.pen, 1)
-    g.vector.tensor_tensor_scan(T.best[:, 1:8:2], T.pen[:], T.idx[:], BIG, AluOpType.min,
-                                AluOpType.max).then_inc(T.sem.fin, 1)
-    g.sync.wait_ge(T.sem.fin, 1)
-    g.sync.dma_start(T.y[:], T.best[:, 6:8]).then_inc(T.sem.st, 16)
-    g.sync.wait_ge(T.sem.st, 16)
+    top = T.land[:, 0:n * PAIR:PAIR]
+    g.vector.wait_ge(sem.const, n + 2)
+    g.vector.wait_ge(sem.own, 1)
+    g.vector.wait_ge(sem.pair, len(far_es))
+    g.vector.wait_ge(sem.top, late)
+    g.vector.tensor_reduce(T.best[:, 22:23], top, AxisListType.X, AluOpType.max).then_inc(sem.gmax, 1)
+    g.vector.wait_ge(sem.gmax, 1)
+    for j, pen in ((0, -BIG), (1, BIG)):
+        g.vector.tensor_scalar(T.step[:, j:12:3], top, T.best[:, 22:23], pen, AluOpType.is_lt,
+                               AluOpType.mult).then_inc(sem.step, 1)
+    g.vector.wait_ge(sem.step, 2)
+    g.vector.wait_ge(sem.res, late)
+    g.vector.tensor_tensor_scan(T.best[:, 1:24:2], T.step[:], T.land[:, 1:n * PAIR:4], NONE, AluOpType.add,
+                                AluOpType.min).then_inc(sem.fin, 1)
+    g.sync.wait_ge(sem.fin, 1)
+    g.sync.dma_start(T.y[:], T.best[:, 22:24]).then_inc(sem.st, 16)
+    g.sync.wait_ge(sem.st, 16)

from concourse.bass import DstId, RemoteDMATransfer
from concourse.mybir import dt, AluOpType, AxisListType, ActivationFunctionType

NT = 128
NC = 384
HALF = 192
SLOT = 400
PAIR = 12
BIG = 8192.0
NONE = 4 * BIG
LOW = -1.0e29

SCRATCH = {
    "xt": ("sbuf", [128, 4 * NT], "bfloat16"),
    "wt": ("sbuf", [128, 4 * NC], "bfloat16"),
    "xc": ("sbuf", [128, 4 * NT], "float8_e4m3fn_x4"),
    "xs": ("sbuf", [128, 4 * NT], "uint8"),
    "wc": ("sbuf", [128, NC], "float8_e4m3fn_x4"),
    "ws": ("sbuf", [128, NC], "uint8"),
    "ps": ("psum", [128, 5 * 512], "float32"),
    "low": ("sbuf", [128, NC], "bfloat16"),
    "run": ("sbuf", [128, 4 * SLOT], "float32"),
    "junk": ("sbuf", [128, 4 * NC], "bfloat16"),
    "land": ("sbuf", [128, 4 * PAIR], "float32"),
    "step": ("sbuf", [128, 12], "float32"),
    "best": ("sbuf", [128, 24], "float32"),
}
SEMAPHORES = (["ldx", "ldw", "qx", "qw", "low", "const", "sent", "own", "pair", "top", "res", "gmax", "step", "fin",
               "st", "mmh", "sch"]
              + ["arr%d" % k for k in range(4)] + ["mm%d" % k for k in range(4)]
              + ["sc%d" % k for k in range(4)] + ["ac%d" % k for k in range(4)])


def rank_program(g, core, T, topo):
    me = T.rank_of(core)
    if me is None:
        return
    cores = T.cores
    n = len(cores)
    sem = T.sem

    def dst(c):
        rid, pid, _ = topo.addr(c)
        return DstId(rid=rid, pnc=pid)

    def engines(m):
        return [e for e in range(m.bit_length()) if (m >> e) & 1]

    def mask(es):
        return sum(1 << e for e in es)

    others = [r for r in range(n) if r != me]
    near = [r for r in others if topo.chip(cores[r]) == topo.chip(core)]
    far = [r for r in others if r not in near]
    far.sort(key=lambda r: topo.die(cores[r]) != topo.die(core))
    near, (far1, far2) = near[0], far
    far_es = engines(topo.mask(core, cores[far1]))
    near_es = [e for e in engines(topo.mask(core, cores[near])) if e not in far_es]
    es = {far1: far_es, far2: far_es, near: near_es}
    order = [me, far1, near, far2]

    def codes(r):
        return T.xc[:, NT * r:NT * (r + 1)]

    def plane(r):
        return T.xs[:, NT * r:NT * (r + 1)]

    def record(r, a, b):
        return T.run[:, SLOT * r + a:SLOT * r + b]

    def send(r, src, out, to):
        return RemoteDMATransfer(dst_ids=[dst(cores[r])], dma_engine_mask=mask(es[r]), remote_sem=to,
                                 srcs=[src], dsts=[out])

    g.sync.dma_start(T.xt[:], T.x[:]).then_inc(sem.ldx, 16)
    g.sync.dma_start(T.wt[:], T.w[:]).then_inc(sem.ldw, 16)

    g.wait_ge(sem.qx, 1)
    sent = 0
    for group in ((far1,), (far2, near)):
        for piece in (codes(me).bitcast(dt.uint8), plane(me)):
            g.remote_dma_fused([send(r, piece, piece, sem["arr%d" % me]) for r in group], local_sem=sem.sent)
            sent += sum(len(es[r]) for r in group)

    g.vector.memset(T.low[:], LOW).then_inc(sem.low, 1)
    g.vector.wait_ge(sem.ldx, 16)
    g.vector.quantize_mx(codes(me), plane(me), T.xt[:]).then_inc(sem.qx, 1)
    for k in range(n):
        g.vector.memset(T.land[:, PAIR * k + 4:PAIR * (k + 1)], NONE).then_inc(sem.const, 1)
    g.vector.memset(T.step[:, 2:11:3], float(-NC)).then_inc(sem.const, 1)
    g.vector.memset(T.step[:, 11:12], float(NC * (n - 1))).then_inc(sem.const, 1)
    g.vector.wait_ge(sem.ldw, 16)
    g.vector.quantize_mx(T.wc[:], T.ws[:], T.wt[:]).then_inc(sem.qw, 1)
    g.vector.wait_ge(sem.low, 1)

    def scan(r, bank, a, b, first, done):
        g.vector.tensor_tensor_scan(record(r, a, b), bank, T.low[:, a:b], first, AluOpType.max,
                                    AluOpType.max).then_inc(done, 1)

    g.tensor.wait_ge(sem.qx, 1)
    g.tensor.wait_ge(sem.qw, 1)
    for k, r in enumerate(order):
        if r != me:
            g.tensor.wait_ge(sem["arr%d" % r], 2 * len(es[r]))
        if r != far2:
            bank = T.ps[:, 512 * k:512 * k + NC]
            g.tensor.matmul_mx(bank, codes(r), plane(r), T.wc[:], T.ws[:], True, True).then_inc(sem["mm%d" % k], 1)
            g.vector.wait_ge(sem["mm%d" % k], 1)
            scan(r, bank, 0, NC, LOW, sem["sc%d" % k])
        else:
            b0, b1 = T.ps[:, 512 * k:512 * k + HALF], T.ps[:, 512 * (k + 1):512 * (k + 1) + NC - HALF]
            g.tensor.matmul_mx(b0, codes(r), plane(r), T.wc[:, 0:HALF], T.ws[:, 0:HALF], True,
                               True).then_inc(sem.mmh, 1)
            g.tensor.matmul_mx(b1, codes(r), plane(r), T.wc[:, HALF:NC], T.ws[:, HALF:NC], True,
                               True).then_inc(sem["mm%d" % k], 1)
            g.vector.wait_ge(sem.mmh, 1)
            scan(r, b0, 0, HALF, LOW, sem.sch)
            g.vector.wait_ge(sem["mm%d" % k], 1)
            g.vector.wait_ge(sem.sch, 1)
            scan(r, b1, HALF, NC, record(r, HALF - 1, HALF), sem["sc%d" % k])
        g.scalar.wait_ge(sem["sc%d" % k], 1)
        g.scalar.activation(T.junk[:, NC * k:NC * (k + 1)], record(r, 0, NC), ActivationFunctionType.Sign,
                            bias=record(r, NC - 1, NC), scale=-1.0,
                            accum_out=record(r, NC, NC + 1)).then_inc(sem["ac%d" % k], 1)
        if r == me:
            g.scalar.wait_ge(sem["ac%d" % k], 1)
            g.scalar.activation(T.land[:, PAIR * me:PAIR * me + 2], record(r, NC - 1, NC + 1),
                                ActivationFunctionType.Copy).then_inc(sem.own, 1)

    at = PAIR * me
    g.wait_ge(sem.ac1, 1)
    g.remote_dma_fused([send(far1, record(far1, NC - 1, NC + 1), T.land[:, at:at + 2], sem.pair)],
                       local_sem=sem.sent)
    g.wait_ge(sem.sc2, 1)
    g.wait_ge(sem.sc3, 1)
    g.remote_dma_fused([send(r, record(r, NC - 1, NC), T.land[:, at:at + 1], sem.top) for r in (far2, near)],
                       local_sem=sem.sent)
    g.wait_ge(sem.ac2, 1)
    g.wait_ge(sem.ac3, 1)
    g.remote_dma_fused([send(r, record(r, NC, NC + 1), T.land[:, at + 1:at + 2], sem.res) for r in (far2, near)],
                       local_sem=sem.sent)
    late = len(far_es) + len(near_es)
    g.wait_ge(sem.sent, sent + len(far_es) + 2 * late)

    top = T.land[:, 0:n * PAIR:PAIR]
    g.vector.wait_ge(sem.const, n + 2)
    g.vector.wait_ge(sem.own, 1)
    g.vector.wait_ge(sem.pair, len(far_es))
    g.vector.wait_ge(sem.top, late)
    g.vector.tensor_reduce(T.best[:, 22:23], top, AxisListType.X, AluOpType.max).then_inc(sem.gmax, 1)
    g.vector.wait_ge(sem.gmax, 1)
    for j, pen in ((0, -BIG), (1, BIG)):
        g.vector.tensor_scalar(T.step[:, j:12:3], top, T.best[:, 22:23], pen, AluOpType.is_lt,
                               AluOpType.mult).then_inc(sem.step, 1)
    g.vector.wait_ge(sem.step, 2)
    g.vector.wait_ge(sem.res, late)
    g.vector.tensor_tensor_scan(T.best[:, 1:24:2], T.step[:], T.land[:, 1:n * PAIR:4], NONE, AluOpType.add,
                                AluOpType.min).then_inc(sem.fin, 1)
    g.sync.wait_ge(sem.fin, 1)
    g.sync.dma_start(T.y[:], T.best[:, 22:24]).then_inc(sem.st, 16)
    g.sync.wait_ge(sem.st, 16)
